import numpy as np
import ml_dtypes


def mxq(x, axis, fmt="e4m3"):
    dtype, down = {"e4m3": (ml_dtypes.float8_e4m3fn, 7), "e5m2": (ml_dtypes.float8_e5m2, 14)}[fmt]
    v = np.moveaxis(np.asarray(x, np.float32).astype(ml_dtypes.bfloat16).astype(np.float64), axis, -1)
    blocks = v.reshape(v.shape[:-1] + (-1, 32))
    amax = np.abs(blocks).max(-1, keepdims=True)
    byte = np.maximum(np.where(amax > 0, np.frexp(amax)[1] - 1 + 127, 0) - down, 1)
    scale = np.exp2(byte - 127.0)
    codes = (blocks / scale).astype(np.float32).astype(dtype).astype(np.float64)
    return np.moveaxis((codes * scale).reshape(v.shape), -1, axis)


WIDE = False


def mx_kscale(k):
    if not WIDE:
        return np.ones(k)
    levels = np.array([10, -10, 5, -5, 0])
    if k % 512:
        return np.exp2(np.random.permutation(np.resize(levels, k // 32))).repeat(32)
    a = np.empty((k // 512, 16))
    for p in range(k // 512):
        a[p, :8] = np.random.permutation(np.resize(levels, 8))
        for g in range(8):
            far = levels[np.abs(levels - a[p, g]) >= 10]
            a[p, g + 8] = far[np.random.randint(len(far))]
    return np.exp2(a.ravel()).repeat(32)


def f64(x):
    return np.asarray(x).astype(np.float64)


def striped(idx):
    return np.tile(idx.reshape(-1, 16).T, (8, 1)).astype(np.uint16)


def unstriped(offs):
    return offs[:16].T.reshape(-1).astype(np.int64)


E2M1 = np.array([0.0, 0.5, 1.0, 1.5, 2.0, 3.0, 4.0, 6.0, -0.0, -0.5, -1.0, -1.5, -2.0, -3.0, -4.0, -6.0])


def pack_weight(w, fmt):
    k, n = w.shape
    w = f64(np.asarray(w, np.float32).astype(ml_dtypes.bfloat16)).reshape(k // 32, 32, n)
    amax = np.abs(w).max(1)
    if fmt == "e4m3":
        byte = np.frexp(amax)[1] - 1 + 127 - 7
    else:
        mant, ex = np.frexp(amax / 6.0)
        byte = np.where(mant > 0.5, ex, ex - 1) + 127
    byte = np.clip(np.where(amax > 0, byte, 1), 1, 254)
    scaled = (w * np.exp2(127.0 - byte)[:, None, :]).reshape(k, n).astype(np.float32)
    by_word = np.ascontiguousarray(scaled.reshape(k // 512, 128, 4, n).transpose(0, 1, 3, 2))
    if fmt == "e4m3":
        words = by_word.astype(ml_dtypes.float8_e4m3fn).view(np.uint8)
    else:
        c = by_word.astype(ml_dtypes.float4_e2m1fn).view(np.uint8) & 0xF
        words = (c[..., 0::2] | (c[..., 1::2] << 4)).reshape(k // 512, 128, 2 * n)
    return np.ascontiguousarray(words), np.ascontiguousarray(byte.astype(np.uint8).reshape(k // 512, 16, n))


def unpack_weight(words, scales, fmt):
    g, _, n = scales.shape
    words = np.ascontiguousarray(words).reshape(g, 128, n, -1)
    if fmt == "e4m3":
        vals = words.view(ml_dtypes.float8_e4m3fn).astype(np.float64)
    else:
        nib = np.empty((g, 128, n, 4), np.uint8)
        nib[..., 0::2] = words & 0xF
        nib[..., 1::2] = words >> 4
        vals = E2M1[nib]
    vals = vals * np.repeat(np.exp2(scales.astype(np.float64) - 127.0), 8, axis=1)[..., None]
    return vals.transpose(0, 1, 3, 2).reshape(g * 512, n)


def gelu(v):
    return 0.5 * v * (1.0 + np.tanh(np.sqrt(2.0 / np.pi) * (v + 0.044715 * v**3)))


def striped8(idx):
    return np.concatenate([v.reshape(-1, 16).T for v in idx]).astype(np.uint16)


def unstriped8(offs):
    return np.stack([offs[16 * g:16 * g + 16].T.reshape(-1) for g in range(8)]).astype(np.int64)


def runs(v, idx8):
    k = np.arange(v.shape[0])
    return v[k[:, None], idx8[k % 512 // 64]]


K, T, S, P, H, N = 1536, 2048, 1024, 512, 512, 1024

def setup_inputs():
    n = np.random.standard_normal
    s = mx_kscale(K)[:, None]
    u = mx_kscale(H)[:, None]
    u2 = mx_kscale(N)[:, None]
    tab_words, tab_scales = pack_weight(n((K, T)) * s, "e4m3")
    w1 = n((K, H)) / np.sqrt(K) / s
    w2_words, w2_scales = pack_weight(2.7 * n((H, N)) / np.sqrt(H) / u, "e2m1")
    w3 = 1.2 * n((N, N)) / np.sqrt(N) / u2
    return {
        "tab_words": tab_words, "tab_scales": tab_scales,
        "offs": striped(np.random.permutation(T)[:S]),
        "offs2": striped8(np.stack([np.random.permutation(S)[:P] for _ in range(8)])),
        "w1": w1.astype(np.float32),
        "thr": np.repeat(n(H // 64), 64).astype(np.float32),
        "road": (n((H, P)) * u).astype(np.float32),
        "w2_words": w2_words, "w2_scales": w2_scales,
        "gain": (np.random.uniform(0.5, 2.0, N) * u2[:, 0]).astype(np.float32),
        "w3": w3.astype(np.float32),
        "tilt": n(N).astype(np.float32),
    }

def reference(tab_words, tab_scales, offs, offs2, w1, thr, road, w2_words, w2_scales, gain, w3, tilt):
    v = unpack_weight(tab_words, tab_scales, "e4m3")[:, unstriped(offs)]
    h = mxq(f64(w1), 0, "e4m3").T @ v
    hp = runs(h, unstriped8(offs2))
    a = 1.0 / (1.0 + np.exp(-(hp + f64(thr)[:, None])))
    x = a * f64(road)
    w2 = unpack_weight(w2_words, w2_scales, "e2m1")
    y = w2.T @ mxq(x, 0, "e4m3")
    f = f64(gain)[:, None] * (y / (1.0 + np.exp(-y)))
    deep = mxq(f64(w3), 0, "e4m3").T @ mxq(f, 0, "e4m3")
    plain = f64(tilt)[:, None] * y
    return np.maximum(deep, plain)

@@ -1,0 +1,281 @@
+from contextlib import ExitStack
+
+import concourse.mybir as mybir
+
+K, T, S, M, H, N = 1536, 2048, 1024, 512, 512, 1024
+FLOPS = 2 * K * H * S + 2 * H * N * M + 2 * N * N * M
+
+F32 = mybir.dt.float32
+BF16 = mybir.dt.bfloat16
+I32 = mybir.dt.int32
+U32 = mybir.dt.uint32
+U16 = mybir.dt.uint16
+U8 = mybir.dt.uint8
+FP8X4 = mybir.dt.float8_e4m3fn_x4
+FP4X4 = mybir.dt.float4_e2m1fn_x4
+ACT = mybir.ActivationFunctionType
+ALU = mybir.AluOpType
+
+P = 128
+PACK = 4
+KP = P * PACK
+BANK = 512
+MH = 256
+MC = 128
+
+
+def tile_list_series_roughness_scores_kernel(
+    tc, tab_words, tab_scales, offs, offs2, w1, thr, road, w2_words, w2_scales, gain, w3, tilt, out
+):
+    nc = tc.nc
+    KA = K // KP
+    NB = N // KP
+
+    with ExitStack() as ctx:
+        keep = ctx.enter_context(tc.tile_pool(name="keep", bufs=1))
+        ring = ctx.enter_context(tc.tile_pool(name="ring", bufs=1))
+        psum = ctx.enter_context(tc.psum_pool(name="psum", bufs=1))
+
+        def held(shape, dtype, name):
+            return keep.tile(shape, dtype, name=name, align_bytes=64)
+
+        def bank(index, shape):
+            return psum.tile(shape, F32, name="bank%d" % index, tag="bank%d" % index)
+
+        def load_weight(rows):
+            width = rows.shape[1]
+            raw = ring.tile([P, PACK, width], F32, name="raw", tag="raw", bufs=5, align_bytes=64)
+            nc.sync.dma_start(out=raw[:], in_=rows.rearrange("(p j) c -> p j c", j=PACK))
+            return raw
+
+        def rounded_tile():
+            return ring.tile([P, PACK * KP], BF16, name="rounded", tag="rounded", bufs=3, align_bytes=64)
+
+        def round_weight(copy, rounded, raw, raw_cols, first_m):
+            src = raw[:, :, raw_cols].rearrange("p j (m t) -> p m j t", t=PACK)
+            count = src.shape[1]
+            dst = rounded[:].rearrange("p (t m j) -> p m j t", t=PACK, j=PACK)[:, first_m : first_m + count]
+            copy(out=dst, in_=src)
+
+        def quantize(rounded, width, name):
+            codes = held([P, width], U32, name + "_codes")
+            scales = held([P, width], U8, name + "_scales")
+            nc.vector.quantize_mx(out=codes[:].bitcast(FP8X4), scales=scales[:], in_=rounded)
+            return codes, scales
+
+        tab_plane = held([P, T], U8, "tab_plane")
+        nc.gpsimd.memset(tab_plane[:].bitcast(I32), 0)
+        for q in range(4):
+            nc.gpsimd.dma_start(
+                out=tab_plane[32 * q : 32 * q + 4 * KA, :].bitcast(I32),
+                in_=tab_scales[:, 4 * q : 4 * q + 4, :].bitcast(I32),
+            )
+        w2_plane_raw = held([P, N], U8, "w2_plane_raw")
+        nc.gpsimd.memset(w2_plane_raw[:].bitcast(I32), 0)
+        for q in range(4):
+            nc.gpsimd.dma_start(
+                out=w2_plane_raw[32 * q : 32 * q + 4, :].bitcast(I32),
+                in_=w2_scales[0, 4 * q : 4 * q + 4, :].bitcast(I32),
+            )
+        idx = held([P, S // 16], U16, "idx")
+        nc.sync.dma_start(idx[:], offs)
+
+        tab = [keep.tile([P, T], U32, name="tab%d" % a, tag="tab%d" % a, align_bytes=64) for a in range(KA)]
+
+        def load_tab(a):
+            nc.sync.dma_start(
+                out=tab[a][:].bitcast(I32), in_=tab_words[a].rearrange("p t i -> p (t i)").bitcast(I32)
+            )
+
+        load_tab(0)
+        w1_raw0 = load_weight(w1[0:KP, :])
+        load_tab(1)
+        w2_raw = held([P, N], U16, "w2_raw")
+        nc.sync.dma_start(out=w2_raw[:].bitcast(I32), in_=w2_words[0].bitcast(I32))
+        load_tab(2)
+        w1_raw1 = load_weight(w1[KP : 2 * KP, :])
+        w1_raw2 = [load_weight(w1[2 * KP : 3 * KP, u * 256 : (u + 1) * 256]) for u in range(2)]
+        idx2 = held([P, M // 16], U16, "idx2")
+        nc.sync.dma_start(idx2[:], offs2)
+        thr_sb = held([P, PACK], F32, "thr_sb")
+        nc.sync.dma_start(out=thr_sb[:], in_=thr.rearrange("(p i) -> p i", i=PACK))
+        road_sb = held([P, PACK, M], F32, "road_sb")
+        nc.sync.dma_start(out=road_sb[:], in_=road.rearrange("(p i) m -> p i m", i=PACK))
+        gain_sb = held([P, NB, PACK], F32, "gain_sb")
+        nc.sync.dma_start(out=gain_sb[:], in_=gain.rearrange("(b p i) -> p b i", p=P, i=PACK))
+        tilt_sb = held([P, NB, PACK], F32, "tilt_sb")
+        nc.sync.dma_start(out=tilt_sb[:], in_=tilt.rearrange("(b p i) -> p b i", p=P, i=PACK))
+        w3_raw = {}
+        for b in range(NB):
+            for kb in range(NB):
+                w3_raw[kb, b] = load_weight(w3[kb * KP : (kb + 1) * KP, b * KP : (b + 1) * KP])
+
+        v_words = [held([P, S], U32, "v_words%d" % a) for a in range(KA)]
+        h_banks = [[bank(2 * i + u, [P, BANK]) for u in range(2)] for i in range(PACK)]
+
+        def gather_words(a):
+            nc.vector.tensor_copy(out=v_words[a][:], in_=tab[a][:].indirect(idx[:]))
+
+        def h_pass(a, w1_q):
+            codes, scales = w1_q
+            for i in range(PACK):
+                for u in range(2):
+                    cols = slice(u * BANK, (u + 1) * BANK)
+                    nc.tensor.matmul_mx(
+                        out=h_banks[i][u][:],
+                        lhsT=codes[:, i * P : (i + 1) * P].bitcast(FP8X4),
+                        lhsT_scale=scales[:, i * P : (i + 1) * P],
+                        rhs=v_words[a][:, cols].bitcast(FP8X4),
+                        rhs_scale=v_plane[4 * a : P, cols],
+                        start=(a == 0),
+                        stop=(a == KA - 1),
+                    )
+
+        gather_words(0)
+        v_plane = keep.tile([P, S], U8, name="v_plane", tag="tab0", align_bytes=64)
+        nc.vector.tensor_copy(out=v_plane[:], in_=tab_plane[:].indirect(idx[:]))
+        r0 = rounded_tile()
+        round_weight(nc.scalar.copy, r0, w1_raw0, slice(0, KP), 0)
+        h_pass(0, quantize(r0[:], KP, "w1_0"))
+        gather_words(1)
+
+        w2_codes = held([P, N], U16, "w2_codes")
+        nc.scalar.copy(
+            out=w2_codes[:].rearrange("p (b t m) -> p b m t", b=NB, t=PACK),
+            in_=w2_raw[:].rearrange("p (b m t) -> p b m t", b=NB, t=PACK),
+        )
+        w2_plane = held([P, N], U8, "w2_plane")
+        nc.vector.tensor_copy(
+            out=w2_plane[:].rearrange("p (b t m) -> p b t m", b=NB, t=PACK),
+            in_=w2_plane_raw[:].rearrange("p (b m t) -> p b t m", b=NB, t=PACK),
+        )
+
+        gather_words(2)
+        r1 = rounded_tile()
+        round_weight(nc.scalar.copy, r1, w1_raw1, slice(0, 256), 0)
+        round_weight(nc.vector.tensor_copy, r1, w1_raw1, slice(256, KP), 64)
+        h_pass(1, quantize(r1[:], KP, "w1_1"))
+        r2 = rounded_tile()
+        round_weight(nc.scalar.copy, r2, w1_raw2[0], slice(0, 256), 0)
+        round_weight(nc.vector.tensor_copy, r2, w1_raw2[1], slice(0, 256), 64)
+        h_pass(2, quantize(r2[:], KP, "w1_2"))
+
+        h = [held([P, S], F32, "h%d" % i) for i in range(PACK)]
+        for i in range(PACK):
+            for u in range(2):
+                nc.vector.tensor_copy(out=h[i][:, u * BANK : (u + 1) * BANK], in_=h_banks[i][u][:])
+        gates = [held([P, PACK, MH], F32, "gates%d" % mh) for mh in range(2)]
+        for mh in range(2):
+            for i in range(PACK):
+                nc.scalar.activation(
+                    out=gates[mh][:, i, :],
+                    in_=h[i][:].indirect(idx2[:, mh * (MH // 16) : (mh + 1) * (MH // 16)]),
+                    func=ACT.Sigmoid,
+                    bias=thr_sb[:, i : i + 1],
+                )
+
+        w3_q = {}
+
+        def prepare_w3(kb, b, copy):
+            r = rounded_tile()
+            round_weight(copy, r, w3_raw[kb, b], slice(0, KP), 0)
+            w3_q[kb, b] = quantize(r[:], KP, "w3_%d_%d" % (kb, b))
+
+        y_sb = [held([P, NB, PACK, MH], F32, "y_sb%d" % mh) for mh in range(2)]
+        y_banks = {}
+        for mh in range(2):
+            x_bf = held([P, MH * PACK], BF16, "x_bf%d" % mh)
+            nc.vector.tensor_tensor(
+                out=x_bf[:].rearrange("p (c e t) -> p c t e", e=4, t=PACK),
+                in0=gates[mh][:].rearrange("p t (c e) -> p c t e", e=4),
+                in1=road_sb[:, :, mh * MH : (mh + 1) * MH].rearrange("p t (c e) -> p c t e", e=4),
+                op=ALU.mult,
+            )
+            x_codes, x_scales = quantize(x_bf[:], MH, "x%d" % mh)
+            for b in range(NB):
+                for mc in range(2):
+                    cols = slice(mc * MC, (mc + 1) * MC)
+                    yb = bank(4 * mh + 2 * b + mc, [P, PACK, MC])
+                    y_banks[mh, mc, b] = yb
+                    for i in range(PACK):
+                        c0 = b * KP + i * P
+                        nc.tensor.matmul_mx(
+                            out=yb[:, i, :],
+                            lhsT=w2_codes[:, c0 : c0 + P].bitcast(FP4X4),
+                            lhsT_scale=w2_plane[:, c0 : c0 + P],
+                            rhs=x_codes[:, cols].bitcast(FP8X4),
+                            rhs_scale=x_scales[:, cols],
+                            start=True,
+                            stop=True,
+                        )
+
+        f_q = {}
+
+        def f_part(mh, b):
+            silu = ring.tile([P, MH, PACK], F32, name="silu", tag="silu", bufs=4, align_bytes=64)
+            f_bf = ring.tile([P, MH, PACK], BF16, name="f_bf", tag="f_bf", bufs=4, align_bytes=64)
+            for mc in range(2):
+                nc.scalar.activation(
+                    out=silu[:, mc * MC : (mc + 1) * MC, :],
+                    in_=y_banks[mh, mc, b][:].rearrange("p i m -> p m i"),
+                    func=ACT.Silu,
+                )
+            nc.vector.tensor_tensor(
+                out=f_bf[:],
+                in0=silu[:],
+                in1=gain_sb[:, b, :].unsqueeze(1).to_broadcast([P, MH, PACK]),
+                op=ALU.mult,
+            )
+            f_q[mh, b] = quantize(f_bf[:].rearrange("p m i -> p (m i)"), MH, "f%d_%d" % (mh, b))
+
+        def y_out(mh, b):
+            for mc in range(2):
+                nc.scalar.copy(out=y_sb[mh][:, b, :, mc * MC : (mc + 1) * MC], in_=y_banks[mh, mc, b][:])
+
+        def deep(mh, b):
+            for pair in range(2):
+                acc = bank(4 * mh + 2 * b + pair, [P, 2, MH])
+                res = ring.tile([P, 2, MH], F32, name="res", tag="res", bufs=8, align_bytes=64)
+                for e in range(2):
+                    i = 2 * pair + e
+                    for kb in range(NB):
+                        codes, scales = w3_q[kb, b]
+                        f_codes, f_scales = f_q[mh, kb]
+                        nc.tensor.matmul_mx(
+                            out=acc[:, e, :],
+                            lhsT=codes[:, i * P : (i + 1) * P].bitcast(FP8X4),
+                            lhsT_scale=scales[:, i * P : (i + 1) * P],
+                            rhs=f_codes[:].bitcast(FP8X4),
+                            rhs_scale=f_scales[:],
+                            start=(kb == 0),
+                            stop=(kb == NB - 1),
+                        )
+                for e in range(2):
+                    i = 2 * pair + e
+                    nc.vector.scalar_tensor_tensor(
+                        out=res[:, e, :],
+                        in0=y_sb[mh][:, b, i, :],
+                        scalar=tilt_sb[:, b, i : i + 1],
+                        in1=acc[:, e, :],
+                        op0=ALU.mult,
+                        op1=ALU.max,
+                    )
+                rows = out[b * KP : (b + 1) * KP, mh * MH : (mh + 1) * MH].rearrange("(p i) m -> p i m", i=PACK)
+                nc.sync.dma_start(out=rows[:, 2 * pair : 2 * pair + 2, :], in_=res[:])
+
+        prepare_w3(0, 0, nc.vector.tensor_copy)
+        f_part(0, 0)
+        f_part(0, 1)
+        y_out(0, 0)
+        prepare_w3(1, 0, nc.vector.tensor_copy)
+        f_part(1, 0)
+        f_part(1, 1)
+        y_out(1, 0)
+        deep(0, 0)
+        prepare_w3(0, 1, nc.scalar.copy)
+        y_out(0, 1)
+        deep(1, 0)
+        prepare_w3(1, 1, nc.scalar.copy)
+        y_out(1, 1)
+        deep(0, 1)
+        deep(1, 1)

@@ -44,7 +44,7 @@ def tile_list_series_roughness_scores_kernel(
 
         def load_weight(rows):
             width = rows.shape[1]
-            raw = ring.tile([P, PACK, width], F32, name="raw", tag="raw", bufs=5, align_bytes=64)
+            raw = ring.tile([P, PACK, width], F32, name="raw", tag="raw", bufs=6, align_bytes=64)
             nc.sync.dma_start(out=raw[:], in_=rows.rearrange("(p j) c -> p j c", j=PACK))
             return raw
 
@@ -64,19 +64,9 @@ def tile_list_series_roughness_scores_kernel(
             return codes, scales
 
         tab_plane = held([P, T], U8, "tab_plane")
-        nc.gpsimd.memset(tab_plane[:].bitcast(I32), 0)
-        for q in range(4):
-            nc.gpsimd.dma_start(
-                out=tab_plane[32 * q : 32 * q + 4 * KA, :].bitcast(I32),
-                in_=tab_scales[:, 4 * q : 4 * q + 4, :].bitcast(I32),
-            )
+        nc.vector.memset(tab_plane[:].bitcast(I32), 0)
         w2_plane_raw = held([P, N], U8, "w2_plane_raw")
-        nc.gpsimd.memset(w2_plane_raw[:].bitcast(I32), 0)
-        for q in range(4):
-            nc.gpsimd.dma_start(
-                out=w2_plane_raw[32 * q : 32 * q + 4, :].bitcast(I32),
-                in_=w2_scales[0, 4 * q : 4 * q + 4, :].bitcast(I32),
-            )
+        nc.vector.memset(w2_plane_raw[:].bitcast(I32), 0)
         idx = held([P, S // 16], U16, "idx")
         nc.sync.dma_start(idx[:], offs)
 
@@ -89,26 +79,41 @@ def tile_list_series_roughness_scores_kernel(
 
         load_tab(0)
         w1_raw0 = load_weight(w1[0:KP, :])
-        load_tab(1)
-        w2_raw = held([P, N], U16, "w2_raw")
-        nc.sync.dma_start(out=w2_raw[:].bitcast(I32), in_=w2_words[0].bitcast(I32))
-        load_tab(2)
-        w1_raw1 = load_weight(w1[KP : 2 * KP, :])
-        w1_raw2 = [load_weight(w1[2 * KP : 3 * KP, u * 256 : (u + 1) * 256]) for u in range(2)]
         idx2 = held([P, M // 16], U16, "idx2")
         nc.sync.dma_start(idx2[:], offs2)
         thr_sb = held([P, PACK], F32, "thr_sb")
         nc.sync.dma_start(out=thr_sb[:], in_=thr.rearrange("(p i) -> p i", i=PACK))
+        for q in range(4):
+            nc.sync.dma_start(
+                out=tab_plane[32 * q : 32 * q + 4 * KA, :].bitcast(I32),
+                in_=tab_scales[:, 4 * q : 4 * q + 4, :].bitcast(I32),
+            )
+        load_tab(1)
+        w1_raw1 = load_weight(w1[KP : 2 * KP, :])
+        load_tab(2)
+        w1_raw2 = load_weight(w1[2 * KP : 3 * KP, :])
+        w2_raw = held([P, N], U16, "w2_raw")
+        nc.sync.dma_start(out=w2_raw[:].bitcast(I32), in_=w2_words[0].bitcast(I32))
+        for q in range(4):
+            nc.sync.dma_start(
+                out=w2_plane_raw[32 * q : 32 * q + 4, :].bitcast(I32),
+                in_=w2_scales[0, 4 * q : 4 * q + 4, :].bitcast(I32),
+            )
+        w3_raw = {}
+
+        def load_w3(kb, b):
+            w3_raw[kb, b] = load_weight(w3[kb * KP : (kb + 1) * KP, b * KP : (b + 1) * KP])
+
+        load_w3(0, 0)
         road_sb = held([P, PACK, M], F32, "road_sb")
         nc.sync.dma_start(out=road_sb[:], in_=road.rearrange("(p i) m -> p i m", i=PACK))
         gain_sb = held([P, NB, PACK], F32, "gain_sb")
         nc.sync.dma_start(out=gain_sb[:], in_=gain.rearrange("(b p i) -> p b i", p=P, i=PACK))
         tilt_sb = held([P, NB, PACK], F32, "tilt_sb")
         nc.sync.dma_start(out=tilt_sb[:], in_=tilt.rearrange("(b p i) -> p b i", p=P, i=PACK))
-        w3_raw = {}
-        for b in range(NB):
-            for kb in range(NB):
-                w3_raw[kb, b] = load_weight(w3[kb * KP : (kb + 1) * KP, b * KP : (b + 1) * KP])
+        load_w3(1, 0)
+        load_w3(0, 1)
+        load_w3(1, 1)
 
         v_words = [held([P, S], U32, "v_words%d" % a) for a in range(KA)]
         h_banks = [[bank(2 * i + u, [P, BANK]) for u in range(2)] for i in range(PACK)]
@@ -138,6 +143,35 @@ def tile_list_series_roughness_scores_kernel(
         round_weight(nc.scalar.copy, r0, w1_raw0, slice(0, KP), 0)
         h_pass(0, quantize(r0[:], KP, "w1_0"))
         gather_words(1)
+        r1 = rounded_tile()
+        round_weight(nc.scalar.copy, r1, w1_raw1, slice(0, 256), 0)
+        round_weight(nc.vector.tensor_copy, r1, w1_raw1, slice(256, KP), 64)
+        h_pass(1, quantize(r1[:], KP, "w1_1"))
+        gather_words(2)
+        r2 = rounded_tile()
+        round_weight(nc.scalar.copy, r2, w1_raw2, slice(0, 224), 0)
+        round_weight(nc.vector.tensor_copy, r2, w1_raw2, slice(224, KP), 56)
+        h_pass(2, quantize(r2[:], KP, "w1_2"))
+
+        h = [held([P, S], F32, "h%d" % i) for i in range(PACK)]
+        gates = [held([P, PACK, MH], F32, "gates%d" % mh) for mh in range(2)]
+
+        def h_out(i, u, copy):
+            copy(out=h[i][:, u * BANK : (u + 1) * BANK], in_=h_banks[i][u][:])
+
+        def look(i):
+            for mh in range(2):
+                nc.scalar.activation(
+                    out=gates[mh][:, i, :],
+                    in_=h[i][:].indirect(idx2[:, mh * (MH // 16) : (mh + 1) * (MH // 16)]),
+                    func=ACT.Sigmoid,
+                    bias=thr_sb[:, i : i + 1],
+                )
+
+        for i in range(PACK):
+            h_out(i, 0, nc.vector.tensor_copy)
+            h_out(i, 1, nc.vector.tensor_copy)
+            look(i)
 
         w2_codes = held([P, N], U16, "w2_codes")
         nc.scalar.copy(
@@ -150,30 +184,6 @@ def tile_list_series_roughness_scores_kernel(
             in_=w2_plane_raw[:].rearrange("p (b m t) -> p b t m", b=NB, t=PACK),
         )
 
-        gather_words(2)
-        r1 = rounded_tile()
-        round_weight(nc.scalar.copy, r1, w1_raw1, slice(0, 256), 0)
-        round_weight(nc.vector.tensor_copy, r1, w1_raw1, slice(256, KP), 64)
-        h_pass(1, quantize(r1[:], KP, "w1_1"))
-        r2 = rounded_tile()
-        round_weight(nc.scalar.copy, r2, w1_raw2[0], slice(0, 256), 0)
-        round_weight(nc.vector.tensor_copy, r2, w1_raw2[1], slice(0, 256), 64)
-        h_pass(2, quantize(r2[:], KP, "w1_2"))
-
-        h = [held([P, S], F32, "h%d" % i) for i in range(PACK)]
-        for i in range(PACK):
-            for u in range(2):
-                nc.vector.tensor_copy(out=h[i][:, u * BANK : (u + 1) * BANK], in_=h_banks[i][u][:])
-        gates = [held([P, PACK, MH], F32, "gates%d" % mh) for mh in range(2)]
-        for mh in range(2):
-            for i in range(PACK):
-                nc.scalar.activation(
-                    out=gates[mh][:, i, :],
-                    in_=h[i][:].indirect(idx2[:, mh * (MH // 16) : (mh + 1) * (MH // 16)]),
-                    func=ACT.Sigmoid,
-                    bias=thr_sb[:, i : i + 1],
-                )
-
         w3_q = {}
 
         def prepare_w3(kb, b, copy):
@@ -181,7 +191,7 @@ def tile_list_series_roughness_scores_kernel(
             round_weight(copy, r, w3_raw[kb, b], slice(0, KP), 0)
             w3_q[kb, b] = quantize(r[:], KP, "w3_%d_%d" % (kb, b))
 
-        y_sb = [held([P, NB, PACK, MH], F32, "y_sb%d" % mh) for mh in range(2)]
+        y_sb = [held([P, PACK, M], F32, "y_sb%d" % b) for b in range(NB)]
         y_banks = {}
         for mh in range(2):
             x_bf = held([P, MH * PACK], BF16, "x_bf%d" % mh)
@@ -195,7 +205,7 @@ def tile_list_series_roughness_scores_kernel(
             for b in range(NB):
                 for mc in range(2):
                     cols = slice(mc * MC, (mc + 1) * MC)
-                    yb = bank(4 * mh + 2 * b + mc, [P, PACK, MC])
+                    yb = bank(4 * b + 2 * mh + mc, [P, PACK, MC])
                     y_banks[mh, mc, b] = yb
                     for i in range(PACK):
                         c0 = b * KP + i * P
@@ -230,52 +240,52 @@ def tile_list_series_roughness_scores_kernel(
 
         def y_out(mh, b):
             for mc in range(2):
-                nc.scalar.copy(out=y_sb[mh][:, b, :, mc * MC : (mc + 1) * MC], in_=y_banks[mh, mc, b][:])
+                m0 = mh * MH + mc * MC
+                nc.scalar.copy(out=y_sb[b][:, :, m0 : m0 + MC], in_=y_banks[mh, mc, b][:])
 
-        def deep(mh, b):
-            for pair in range(2):
-                acc = bank(4 * mh + 2 * b + pair, [P, 2, MH])
-                res = ring.tile([P, 2, MH], F32, name="res", tag="res", bufs=8, align_bytes=64)
-                for e in range(2):
-                    i = 2 * pair + e
-                    for kb in range(NB):
-                        codes, scales = w3_q[kb, b]
-                        f_codes, f_scales = f_q[mh, kb]
-                        nc.tensor.matmul_mx(
-                            out=acc[:, e, :],
-                            lhsT=codes[:, i * P : (i + 1) * P].bitcast(FP8X4),
-                            lhsT_scale=scales[:, i * P : (i + 1) * P],
-                            rhs=f_codes[:].bitcast(FP8X4),
-                            rhs_scale=f_scales[:],
-                            start=(kb == 0),
-                            stop=(kb == NB - 1),
-                        )
-                for e in range(2):
-                    i = 2 * pair + e
-                    nc.vector.scalar_tensor_tensor(
-                        out=res[:, e, :],
-                        in0=y_sb[mh][:, b, i, :],
-                        scalar=tilt_sb[:, b, i : i + 1],
-                        in1=acc[:, e, :],
-                        op0=ALU.mult,
-                        op1=ALU.max,
-                    )
-                rows = out[b * KP : (b + 1) * KP, mh * MH : (mh + 1) * MH].rearrange("(p i) m -> p i m", i=PACK)
-                nc.sync.dma_start(out=rows[:, 2 * pair : 2 * pair + 2, :], in_=res[:])
+        def deep(acc, mh, b, i):
+            for kb in range(NB):
+                codes, scales = w3_q[kb, b]
+                f_codes, f_scales = f_q[mh, kb]
+                nc.tensor.matmul_mx(
+                    out=acc[:, mh * MH : (mh + 1) * MH],
+                    lhsT=codes[:, i * P : (i + 1) * P].bitcast(FP8X4),
+                    lhsT_scale=scales[:, i * P : (i + 1) * P],
+                    rhs=f_codes[:].bitcast(FP8X4),
+                    rhs_scale=f_scales[:],
+                    start=(kb == 0),
+                    stop=(kb == NB - 1),
+                )
+
+        def finish(b):
+            rows = out[b * KP : (b + 1) * KP, :].rearrange("(p i) m -> p i m", i=PACK)
+            accs = [bank(4 * b + i, [P, M]) for i in range(PACK)]
+            for i in range(PACK):
+                for mh in range(2):
+                    deep(accs[i], mh, b, i)
+            for i in range(PACK):
+                res = ring.tile([P, M], F32, name="res", tag="res", bufs=8, align_bytes=64)
+                nc.vector.scalar_tensor_tensor(
+                    out=res[:],
+                    in0=y_sb[b][:, i, :],
+                    scalar=tilt_sb[:, b, i : i + 1],
+                    in1=accs[i][:],
+                    op0=ALU.mult,
+                    op1=ALU.max,
+                )
+                nc.sync.dma_start(out=rows[:, i, :], in_=res[:])
 
         prepare_w3(0, 0, nc.vector.tensor_copy)
         f_part(0, 0)
         f_part(0, 1)
-        y_out(0, 0)
         prepare_w3(1, 0, nc.vector.tensor_copy)
         f_part(1, 0)
         f_part(1, 1)
-        y_out(1, 0)
-        deep(0, 0)
         prepare_w3(0, 1, nc.scalar.copy)
-        y_out(0, 1)
-        deep(1, 0)
+        y_out(0, 0)
+        y_out(1, 0)
         prepare_w3(1, 1, nc.scalar.copy)
+        finish(0)
+        y_out(0, 1)
         y_out(1, 1)
-        deep(0, 1)
-        deep(1, 1)
+        finish(1)

@@ -48,14 +48,14 @@ def tile_list_series_roughness_scores_kernel(
             nc.sync.dma_start(out=raw[:], in_=rows.rearrange("(p j) c -> p j c", j=PACK))
             return raw
 
-        def rounded_tile():
-            return ring.tile([P, PACK * KP], BF16, name="rounded", tag="rounded", bufs=3, align_bytes=64)
-
-        def round_weight(copy, rounded, raw, raw_cols, first_m):
-            src = raw[:, :, raw_cols].rearrange("p j (m t) -> p m j t", t=PACK)
-            count = src.shape[1]
-            dst = rounded[:].rearrange("p (t m j) -> p m j t", t=PACK, j=PACK)[:, first_m : first_m + count]
+        def prepare_weight(copy, raw, first_pair, pairs, name, tag="rounded", bufs=4):
+            width = pairs * 2 * P
+            rounded = ring.tile([P, PACK * width], BF16, name="rounded", tag=tag, bufs=bufs, align_bytes=64)
+            src = raw[:].rearrange("p j (m u e) -> p u m j e", u=2, e=2)[:, first_pair : first_pair + pairs]
+            dst = rounded[:].rearrange("p (u e m j) -> p u m j e", u=pairs, e=2, j=PACK)
             copy(out=dst, in_=src)
+            codes, scales = quantize(rounded[:], width, name)
+            return [(codes[:, c : c + P], scales[:, c : c + P]) for c in range(0, width, P)]
 
         def quantize(rounded, width, name):
             codes = held([P, width], U32, name + "_codes")
@@ -111,8 +111,8 @@ def tile_list_series_roughness_scores_kernel(
         nc.sync.dma_start(out=gain_sb[:], in_=gain.rearrange("(b p i) -> p b i", p=P, i=PACK))
         tilt_sb = held([P, NB, PACK], F32, "tilt_sb")
         nc.sync.dma_start(out=tilt_sb[:], in_=tilt.rearrange("(b p i) -> p b i", p=P, i=PACK))
-        load_w3(1, 0)
         load_w3(0, 1)
+        load_w3(1, 0)
         load_w3(1, 1)
 
         v_words = [held([P, S], U32, "v_words%d" % a) for a in range(KA)]
@@ -122,14 +122,13 @@ def tile_list_series_roughness_scores_kernel(
             nc.vector.tensor_copy(out=v_words[a][:], in_=tab[a][:].indirect(idx[:]))
 
         def h_pass(a, w1_q):
-            codes, scales = w1_q
-            for i in range(PACK):
+            for i, (codes, scales) in enumerate(w1_q):
                 for u in range(2):
                     cols = slice(u * BANK, (u + 1) * BANK)
                     nc.tensor.matmul_mx(
                         out=h_banks[i][u][:],
-                        lhsT=codes[:, i * P : (i + 1) * P].bitcast(FP8X4),
-                        lhsT_scale=scales[:, i * P : (i + 1) * P],
+                        lhsT=codes.bitcast(FP8X4),
+                        lhsT_scale=scales,
                         rhs=v_words[a][:, cols].bitcast(FP8X4),
                         rhs_scale=v_plane[4 * a : P, cols],
                         start=(a == 0),
@@ -139,21 +138,17 @@ def tile_list_series_roughness_scores_kernel(
         gather_words(0)
         v_plane = keep.tile([P, S], U8, name="v_plane", tag="tab0", align_bytes=64)
         nc.vector.tensor_copy(out=v_plane[:], in_=tab_plane[:].indirect(idx[:]))
-        r0 = rounded_tile()
-        round_weight(nc.scalar.copy, r0, w1_raw0, slice(0, KP), 0)
-        h_pass(0, quantize(r0[:], KP, "w1_0"))
+        h_pass(0, prepare_weight(nc.scalar.copy, w1_raw0, 0, 2, "w1_0"))
         gather_words(1)
-        r1 = rounded_tile()
-        round_weight(nc.scalar.copy, r1, w1_raw1, slice(0, 256), 0)
-        round_weight(nc.vector.tensor_copy, r1, w1_raw1, slice(256, KP), 64)
-        h_pass(1, quantize(r1[:], KP, "w1_1"))
-        gather_words(2)
-        r2 = rounded_tile()
-        round_weight(nc.scalar.copy, r2, w1_raw2, slice(0, 224), 0)
-        round_weight(nc.vector.tensor_copy, r2, w1_raw2, slice(224, KP), 56)
-        h_pass(2, quantize(r2[:], KP, "w1_2"))
+        def prepare_shared(raw, name):
+            low = prepare_weight(nc.vector.tensor_copy, raw, 0, 1, name + "_low")
+            return low + prepare_weight(nc.scalar.copy, raw, 1, 1, name + "_high")
 
-        h = [held([P, S], F32, "h%d" % i) for i in range(PACK)]
+        h_pass(1, prepare_shared(w1_raw1, "w1_1"))
+        gather_words(2)
+        h_pass(2, prepare_shared(w1_raw2, "w1_2"))
+
+        h = [ring.tile([P, S], F32, name="h%d" % i, tag="h%d" % i, bufs=1, align_bytes=64) for i in range(PACK)]
         gates = [held([P, PACK, MH], F32, "gates%d" % mh) for mh in range(2)]
 
         def h_out(i, u, copy):
@@ -175,8 +170,8 @@ def tile_list_series_roughness_scores_kernel(
 
         w2_codes = held([P, N], U16, "w2_codes")
         nc.scalar.copy(
-            out=w2_codes[:].rearrange("p (b t m) -> p b m t", b=NB, t=PACK),
-            in_=w2_raw[:].rearrange("p (b m t) -> p b m t", b=NB, t=PACK),
+            out=w2_codes[:].rearrange("p (b t m) -> p b t m", b=NB, t=PACK),
+            in_=w2_raw[:].rearrange("p (b m t) -> p b t m", b=NB, t=PACK),
         )
         w2_plane = held([P, N], U8, "w2_plane")
         nc.vector.tensor_copy(
@@ -187,9 +182,7 @@ def tile_list_series_roughness_scores_kernel(
         w3_q = {}
 
         def prepare_w3(kb, b, copy):
-            r = rounded_tile()
-            round_weight(copy, r, w3_raw[kb, b], slice(0, KP), 0)
-            w3_q[kb, b] = quantize(r[:], KP, "w3_%d_%d" % (kb, b))
+            w3_q[kb, b] = prepare_weight(copy, w3_raw[kb, b], 0, 2, "w3_%d_%d" % (kb, b))
 
         y_sb = [held([P, PACK, M], F32, "y_sb%d" % b) for b in range(NB)]
         y_banks = {}
@@ -245,35 +238,39 @@ def tile_list_series_roughness_scores_kernel(
 
         def deep(acc, mh, b, i):
             for kb in range(NB):
-                codes, scales = w3_q[kb, b]
+                codes, scales = w3_q[kb, b][i]
                 f_codes, f_scales = f_q[mh, kb]
                 nc.tensor.matmul_mx(
                     out=acc[:, mh * MH : (mh + 1) * MH],
-                    lhsT=codes[:, i * P : (i + 1) * P].bitcast(FP8X4),
-                    lhsT_scale=scales[:, i * P : (i + 1) * P],
+                    lhsT=codes.bitcast(FP8X4),
+                    lhsT_scale=scales,
                     rhs=f_codes[:].bitcast(FP8X4),
                     rhs_scale=f_scales[:],
                     start=(kb == 0),
                     stop=(kb == NB - 1),
                 )
 
-        def finish(b):
+        def finish(b, width):
             rows = out[b * KP : (b + 1) * KP, :].rearrange("(p i) m -> p i m", i=PACK)
-            accs = [bank(4 * b + i, [P, M]) for i in range(PACK)]
-            for i in range(PACK):
-                for mh in range(2):
-                    deep(accs[i], mh, b, i)
-            for i in range(PACK):
-                res = ring.tile([P, M], F32, name="res", tag="res", bufs=8, align_bytes=64)
-                nc.vector.scalar_tensor_tensor(
-                    out=res[:],
-                    in0=y_sb[b][:, i, :],
-                    scalar=tilt_sb[:, b, i : i + 1],
-                    in1=accs[i][:],
-                    op0=ALU.mult,
-                    op1=ALU.max,
-                )
-                nc.sync.dma_start(out=rows[:, i, :], in_=res[:])
+            accs = [bank(i, [P, M]) for i in range(PACK)]
+            groups = [(i, mh) for i in range(PACK) for mh in range(2)]
+            if b == 0:
+                groups = [(i, mh) for mh in range(2) for i in range(PACK)]
+            for i, mh in groups:
+                deep(accs[i], mh, b, i)
+            for m0 in range(0, M, width):
+                cols = slice(m0, m0 + width)
+                for i in range(PACK):
+                    res = ring.tile([P, width], F32, name="res", tag="res", bufs=12, align_bytes=64)
+                    nc.vector.scalar_tensor_tensor(
+                        out=res[:],
+                        in0=y_sb[b][:, i, cols],
+                        scalar=tilt_sb[:, b, i : i + 1],
+                        in1=accs[i][:, cols],
+                        op0=ALU.mult,
+                        op1=ALU.max,
+                    )
+                    nc.sync.dma_start(out=rows[:, i, cols], in_=res[:])
 
         prepare_w3(0, 0, nc.vector.tensor_copy)
         f_part(0, 0)
@@ -281,11 +278,11 @@ def tile_list_series_roughness_scores_kernel(
         prepare_w3(1, 0, nc.vector.tensor_copy)
         f_part(1, 0)
         f_part(1, 1)
-        prepare_w3(0, 1, nc.scalar.copy)
+        w3_q[0, 1] = prepare_weight(nc.scalar.copy, w3_raw[0, 1], 0, 2, "w3_0_1", tag="h3", bufs=1)
         y_out(0, 0)
         y_out(1, 0)
-        prepare_w3(1, 1, nc.scalar.copy)
-        finish(0)
+        w3_q[1, 1] = prepare_shared(w3_raw[1, 1], "w3_1_1")
+        finish(0, M)
         y_out(0, 1)
         y_out(1, 1)
-        finish(1)
+        finish(1, M)

from contextlib import ExitStack

import concourse.mybir as mybir

K, T, S, M, H, N = 1536, 2048, 1024, 512, 512, 1024
FLOPS = 2 * K * H * S + 2 * H * N * M + 2 * N * N * M

F32 = mybir.dt.float32
BF16 = mybir.dt.bfloat16
I32 = mybir.dt.int32
U32 = mybir.dt.uint32
U16 = mybir.dt.uint16
U8 = mybir.dt.uint8
FP8X4 = mybir.dt.float8_e4m3fn_x4
FP4X4 = mybir.dt.float4_e2m1fn_x4
ACT = mybir.ActivationFunctionType
ALU = mybir.AluOpType

P = 128
PACK = 4
KP = P * PACK
BANK = 512
MH = 256
MC = 128


def tile_list_series_roughness_scores_kernel(
    tc, tab_words, tab_scales, offs, offs2, w1, thr, road, w2_words, w2_scales, gain, w3, tilt, out
):
    nc = tc.nc
    KA = K // KP
    NB = N // KP

    with ExitStack() as ctx:
        keep = ctx.enter_context(tc.tile_pool(name="keep", bufs=1))
        ring = ctx.enter_context(tc.tile_pool(name="ring", bufs=1))
        psum = ctx.enter_context(tc.psum_pool(name="psum", bufs=1))

        def held(shape, dtype, name):
            return keep.tile(shape, dtype, name=name, align_bytes=64)

        def bank(index, shape):
            return psum.tile(shape, F32, name="bank%d" % index, tag="bank%d" % index)

        def load_weight(rows):
            width = rows.shape[1]
            raw = ring.tile([P, PACK, width], F32, name="raw", tag="raw", bufs=6, align_bytes=64)
            nc.sync.dma_start(out=raw[:], in_=rows.rearrange("(p j) c -> p j c", j=PACK))
            return raw

        def prepare_weight(copy, raw, first_pair, pairs, name, tag="rounded", bufs=4):
            width = pairs * 2 * P
            rounded = ring.tile([P, PACK * width], BF16, name="rounded", tag=tag, bufs=bufs, align_bytes=64)
            src = raw[:].rearrange("p j (m u e) -> p u m j e", u=2, e=2)[:, first_pair : first_pair + pairs]
            dst = rounded[:].rearrange("p (u e m j) -> p u m j e", u=pairs, e=2, j=PACK)
            copy(out=dst, in_=src)
            codes, scales = quantize(rounded[:], width, name)
            return [(codes[:, c : c + P], scales[:, c : c + P]) for c in range(0, width, P)]

        def quantize(rounded, width, name):
            codes = held([P, width], U32, name + "_codes")
            scales = held([P, width], U8, name + "_scales")
            nc.vector.quantize_mx(out=codes[:].bitcast(FP8X4), scales=scales[:], in_=rounded)
            return codes, scales

        tab_plane = held([P, T], U8, "tab_plane")
        nc.vector.memset(tab_plane[:].bitcast(I32), 0)
        w2_plane_raw = held([P, N], U8, "w2_plane_raw")
        nc.vector.memset(w2_plane_raw[:].bitcast(I32), 0)
        idx = held([P, S // 16], U16, "idx")
        nc.sync.dma_start(idx[:], offs)

        tab = [keep.tile([P, T], U32, name="tab%d" % a, tag="tab%d" % a, align_bytes=64) for a in range(KA)]

        def load_tab(a):
            nc.sync.dma_start(
                out=tab[a][:].bitcast(I32), in_=tab_words[a].rearrange("p t i -> p (t i)").bitcast(I32)
            )

        load_tab(0)
        w1_raw0 = load_weight(w1[0:KP, :])
        idx2 = held([P, M // 16], U16, "idx2")
        nc.sync.dma_start(idx2[:], offs2)
        thr_sb = held([P, PACK], F32, "thr_sb")
        nc.sync.dma_start(out=thr_sb[:], in_=thr.rearrange("(p i) -> p i", i=PACK))
        for q in range(4):
            nc.sync.dma_start(
                out=tab_plane[32 * q : 32 * q + 4 * KA, :].bitcast(I32),
                in_=tab_scales[:, 4 * q : 4 * q + 4, :].bitcast(I32),
            )
        load_tab(1)
        w1_raw1 = load_weight(w1[KP : 2 * KP, :])
        load_tab(2)
        w1_raw2 = load_weight(w1[2 * KP : 3 * KP, :])
        w2_raw = held([P, N], U16, "w2_raw")
        nc.sync.dma_start(out=w2_raw[:].bitcast(I32), in_=w2_words[0].bitcast(I32))
        for q in range(4):
            nc.sync.dma_start(
                out=w2_plane_raw[32 * q : 32 * q + 4, :].bitcast(I32),
                in_=w2_scales[0, 4 * q : 4 * q + 4, :].bitcast(I32),
            )
        w3_raw = {}

        def load_w3(kb, b):
            w3_raw[kb, b] = load_weight(w3[kb * KP : (kb + 1) * KP, b * KP : (b + 1) * KP])

        load_w3(0, 0)
        road_sb = held([P, PACK, M], F32, "road_sb")
        nc.sync.dma_start(out=road_sb[:], in_=road.rearrange("(p i) m -> p i m", i=PACK))
        gain_sb = held([P, NB, PACK], F32, "gain_sb")
        nc.sync.dma_start(out=gain_sb[:], in_=gain.rearrange("(b p i) -> p b i", p=P, i=PACK))
        tilt_sb = held([P, NB, PACK], F32, "tilt_sb")
        nc.sync.dma_start(out=tilt_sb[:], in_=tilt.rearrange("(b p i) -> p b i", p=P, i=PACK))
        load_w3(0, 1)
        load_w3(1, 0)
        load_w3(1, 1)

        v_words = [held([P, S], U32, "v_words%d" % a) for a in range(KA)]
        h_banks = [[bank(2 * i + u, [P, BANK]) for u in range(2)] for i in range(PACK)]

        def gather_words(a):
            nc.vector.tensor_copy(out=v_words[a][:], in_=tab[a][:].indirect(idx[:]))

        def h_pass(a, w1_q):
            for i, (codes, scales) in enumerate(w1_q):
                for u in range(2):
                    cols = slice(u * BANK, (u + 1) * BANK)
                    nc.tensor.matmul_mx(
                        out=h_banks[i][u][:],
                        lhsT=codes.bitcast(FP8X4),
                        lhsT_scale=scales,
                        rhs=v_words[a][:, cols].bitcast(FP8X4),
                        rhs_scale=v_plane[4 * a : P, cols],
                        start=(a == 0),
                        stop=(a == KA - 1),
                    )

        gather_words(0)
        v_plane = keep.tile([P, S], U8, name="v_plane", tag="tab0", align_bytes=64)
        nc.vector.tensor_copy(out=v_plane[:], in_=tab_plane[:].indirect(idx[:]))
        h_pass(0, prepare_weight(nc.scalar.copy, w1_raw0, 0, 2, "w1_0"))
        gather_words(1)
        def prepare_shared(raw, name):
            low = prepare_weight(nc.vector.tensor_copy, raw, 0, 1, name + "_low")
            return low + prepare_weight(nc.scalar.copy, raw, 1, 1, name + "_high")

        h_pass(1, prepare_shared(w1_raw1, "w1_1"))
        gather_words(2)
        h_pass(2, prepare_shared(w1_raw2, "w1_2"))

        h = [ring.tile([P, S], F32, name="h%d" % i, tag="h%d" % i, bufs=1, align_bytes=64) for i in range(PACK)]
        gates = [held([P, PACK, MH], F32, "gates%d" % mh) for mh in range(2)]

        def h_out(i, u, copy):
            copy(out=h[i][:, u * BANK : (u + 1) * BANK], in_=h_banks[i][u][:])

        def look(i):
            for mh in range(2):
                nc.scalar.activation(
                    out=gates[mh][:, i, :],
                    in_=h[i][:].indirect(idx2[:, mh * (MH // 16) : (mh + 1) * (MH // 16)]),
                    func=ACT.Sigmoid,
                    bias=thr_sb[:, i : i + 1],
                )

        for i in range(PACK):
            h_out(i, 0, nc.vector.tensor_copy)
            h_out(i, 1, nc.vector.tensor_copy)
            look(i)

        w2_codes = held([P, N], U16, "w2_codes")
        nc.scalar.copy(
            out=w2_codes[:].rearrange("p (b t m) -> p b t m", b=NB, t=PACK),
            in_=w2_raw[:].rearrange("p (b m t) -> p b t m", b=NB, t=PACK),
        )
        w2_plane = held([P, N], U8, "w2_plane")
        nc.vector.tensor_copy(
            out=w2_plane[:].rearrange("p (b t m) -> p b t m", b=NB, t=PACK),
            in_=w2_plane_raw[:].rearrange("p (b m t) -> p b t m", b=NB, t=PACK),
        )

        w3_q = {}

        def prepare_w3(kb, b, copy):
            w3_q[kb, b] = prepare_weight(copy, w3_raw[kb, b], 0, 2, "w3_%d_%d" % (kb, b))

        y_sb = [held([P, PACK, M], F32, "y_sb%d" % b) for b in range(NB)]
        y_banks = {}
        for mh in range(2):
            x_bf = held([P, MH * PACK], BF16, "x_bf%d" % mh)
            nc.vector.tensor_tensor(
                out=x_bf[:].rearrange("p (c e t) -> p c t e", e=4, t=PACK),
                in0=gates[mh][:].rearrange("p t (c e) -> p c t e", e=4),
                in1=road_sb[:, :, mh * MH : (mh + 1) * MH].rearrange("p t (c e) -> p c t e", e=4),
                op=ALU.mult,
            )
            x_codes, x_scales = quantize(x_bf[:], MH, "x%d" % mh)
            for b in range(NB):
                for mc in range(2):
                    cols = slice(mc * MC, (mc + 1) * MC)
                    yb = bank(4 * b + 2 * mh + mc, [P, PACK, MC])
                    y_banks[mh, mc, b] = yb
                    for i in range(PACK):
                        c0 = b * KP + i * P
                        nc.tensor.matmul_mx(
                            out=yb[:, i, :],
                            lhsT=w2_codes[:, c0 : c0 + P].bitcast(FP4X4),
                            lhsT_scale=w2_plane[:, c0 : c0 + P],
                            rhs=x_codes[:, cols].bitcast(FP8X4),
                            rhs_scale=x_scales[:, cols],
                            start=True,
                            stop=True,
                        )

        f_q = {}

        def f_part(mh, b):
            silu = ring.tile([P, MH, PACK], F32, name="silu", tag="silu", bufs=4, align_bytes=64)
            f_bf = ring.tile([P, MH, PACK], BF16, name="f_bf", tag="f_bf", bufs=4, align_bytes=64)
            for mc in range(2):
                nc.scalar.activation(
                    out=silu[:, mc * MC : (mc + 1) * MC, :],
                    in_=y_banks[mh, mc, b][:].rearrange("p i m -> p m i"),
                    func=ACT.Silu,
                )
            nc.vector.tensor_tensor(
                out=f_bf[:],
                in0=silu[:],
                in1=gain_sb[:, b, :].unsqueeze(1).to_broadcast([P, MH, PACK]),
                op=ALU.mult,
            )
            f_q[mh, b] = quantize(f_bf[:].rearrange("p m i -> p (m i)"), MH, "f%d_%d" % (mh, b))

        def y_out(mh, b):
            for mc in range(2):
                m0 = mh * MH + mc * MC
                nc.scalar.copy(out=y_sb[b][:, :, m0 : m0 + MC], in_=y_banks[mh, mc, b][:])

        def deep(acc, mh, b, i):
            for kb in range(NB):
                codes, scales = w3_q[kb, b][i]
                f_codes, f_scales = f_q[mh, kb]
                nc.tensor.matmul_mx(
                    out=acc[:, mh * MH : (mh + 1) * MH],
                    lhsT=codes.bitcast(FP8X4),
                    lhsT_scale=scales,
                    rhs=f_codes[:].bitcast(FP8X4),
                    rhs_scale=f_scales[:],
                    start=(kb == 0),
                    stop=(kb == NB - 1),
                )

        def finish(b, width):
            rows = out[b * KP : (b + 1) * KP, :].rearrange("(p i) m -> p i m", i=PACK)
            accs = [bank(i, [P, M]) for i in range(PACK)]
            groups = [(i, mh) for i in range(PACK) for mh in range(2)]
            if b == 0:
                groups = [(i, mh) for mh in range(2) for i in range(PACK)]
            for i, mh in groups:
                deep(accs[i], mh, b, i)
            for m0 in range(0, M, width):
                cols = slice(m0, m0 + width)
                for i in range(PACK):
                    res = ring.tile([P, width], F32, name="res", tag="res", bufs=12, align_bytes=64)
                    nc.vector.scalar_tensor_tensor(
                        out=res[:],
                        in0=y_sb[b][:, i, cols],
                        scalar=tilt_sb[:, b, i : i + 1],
                        in1=accs[i][:, cols],
                        op0=ALU.mult,
                        op1=ALU.max,
                    )
                    nc.sync.dma_start(out=rows[:, i, cols], in_=res[:])

        prepare_w3(0, 0, nc.vector.tensor_copy)
        f_part(0, 0)
        f_part(0, 1)
        prepare_w3(1, 0, nc.vector.tensor_copy)
        f_part(1, 0)
        f_part(1, 1)
        w3_q[0, 1] = prepare_weight(nc.scalar.copy, w3_raw[0, 1], 0, 2, "w3_0_1", tag="h3", bufs=1)
        y_out(0, 0)
        y_out(1, 0)
        w3_q[1, 1] = prepare_shared(w3_raw[1, 1], "w3_1_1")
        finish(0, M)
        y_out(0, 1)
        y_out(1, 1)
        finish(1, M)
